import numpy as np
import ml_dtypes


def mxq(x, axis, fmt="e4m3"):
    dtype, down = {"e4m3": (ml_dtypes.float8_e4m3fn, 7), "e5m2": (ml_dtypes.float8_e5m2, 14)}[fmt]
    v = np.moveaxis(np.asarray(x, np.float32).astype(ml_dtypes.bfloat16).astype(np.float64), axis, -1)
    blocks = v.reshape(v.shape[:-1] + (-1, 32))
    amax = np.abs(blocks).max(-1, keepdims=True)
    byte = np.maximum(np.where(amax > 0, np.frexp(amax)[1] - 1 + 127, 0) - down, 1)
    scale = np.exp2(byte - 127.0)
    codes = (blocks / scale).astype(np.float32).astype(dtype).astype(np.float64)
    return np.moveaxis((codes * scale).reshape(v.shape), -1, axis)


WIDE = False


def mx_kscale(k):
    if not WIDE:
        return np.ones(k)
    levels = np.array([10, -10, 5, -5, 0])
    if k % 512:
        return np.exp2(np.random.permutation(np.resize(levels, k // 32))).repeat(32)
    a = np.empty((k // 512, 16))
    for p in range(k // 512):
        a[p, :8] = np.random.permutation(np.resize(levels, 8))
        for g in range(8):
            far = levels[np.abs(levels - a[p, g]) >= 10]
            a[p, g + 8] = far[np.random.randint(len(far))]
    return np.exp2(a.ravel()).repeat(32)


def f64(x):
    return np.asarray(x).astype(np.float64)


def striped(idx):
    return np.tile(np.asarray(idx).reshape(-1, 16).T, (8, 1)).astype(np.uint16)


def unstriped(offs):
    return offs[:16].T.reshape(-1).astype(np.int64)


E2M1 = np.array([0.0, 0.5, 1.0, 1.5, 2.0, 3.0, 4.0, 6.0, -0.0, -0.5, -1.0, -1.5, -2.0, -3.0, -4.0, -6.0])


def pack_weight(w, fmt):
    k, n = w.shape
    w = f64(np.asarray(w, np.float32).astype(ml_dtypes.bfloat16)).reshape(k // 32, 32, n)
    amax = np.abs(w).max(1)
    if fmt == "e4m3":
        byte = np.frexp(amax)[1] - 1 + 127 - 7
    else:
        mant, ex = np.frexp(amax / 6.0)
        byte = np.where(mant > 0.5, ex, ex - 1) + 127
    byte = np.clip(np.where(amax > 0, byte, 1), 1, 254)
    scaled = (w * np.exp2(127.0 - byte)[:, None, :]).reshape(k, n).astype(np.float32)
    by_word = np.ascontiguousarray(scaled.reshape(k // 512, 128, 4, n).transpose(0, 1, 3, 2))
    if fmt == "e4m3":
        words = by_word.astype(ml_dtypes.float8_e4m3fn).view(np.uint8)
    else:
        c = by_word.astype(ml_dtypes.float4_e2m1fn).view(np.uint8) & 0xF
        words = (c[..., 0::2] | (c[..., 1::2] << 4)).reshape(k // 512, 128, 2 * n)
    return np.ascontiguousarray(words), np.ascontiguousarray(byte.astype(np.uint8).reshape(k // 512, 16, n))


def unpack_weight(words, scales, fmt):
    g, _, n = scales.shape
    words = np.ascontiguousarray(words).reshape(g, 128, n, -1)
    if fmt == "e4m3":
        vals = words.view(ml_dtypes.float8_e4m3fn).astype(np.float64)
    else:
        nib = np.empty((g, 128, n, 4), np.uint8)
        nib[..., 0::2] = words & 0xF
        nib[..., 1::2] = words >> 4
        vals = E2M1[nib]
    vals = vals * np.repeat(np.exp2(scales.astype(np.float64) - 127.0), 8, axis=1)[..., None]
    return vals.transpose(0, 1, 3, 2).reshape(g * 512, n)


def sigmoid(v):
    return 1.0 / (1.0 + np.exp(-v))


D, T, I, Q, E, Z, M, C = 512, 2048, 512, 256, 512, 1024, 1024, 512


def setup_inputs():
    n = np.random.standard_normal
    idx = np.random.permutation(T)[:I]
    idx2 = np.random.permutation(Z)[:I]
    idx3 = np.random.permutation(Z)[:I]
    idx4 = np.random.permutation(M)[:Q]
    fd = mx_kscale(D)
    fi = mx_kscale(I)
    fc = mx_kscale(C)
    ti = np.ones(T)
    ti[idx] = fi
    keysp = pack_weight(n((D, T)) / fd[:, None], "e4m3")
    return {
        "query": (n((D, Q)) * 1.0 / np.sqrt(D) * fd[:, None]).astype(np.float32),
        "query2": (n((D, Q)) * 1.0 / np.sqrt(D) * fd[:, None]).astype(np.float32),
        "keys_words": keysp[0],
        "keys_scales": keysp[1],
        "pages": (n((D, Z)) / fd[:, None]).astype(np.float32),
        "os": (np.random.uniform(0.02, 0.08, (1, I)) * fi).astype(np.float32),
        "vals": (n((E, T)) / ti).astype(np.float32),
        "wm": (n((C, E)) * 1.0 / np.sqrt(C) * fc[:, None]).astype(np.float32),
        "mstore": (n((C, M)) / fc[:, None]).astype(np.float32),
        "offs": striped(idx),
        "offs2": striped(idx2),
        "offs3": striped(idx3),
        "offs4": striped(idx4),
    }


def reference(query, query2, keys_words, keys_scales, pages, os, vals, wm, mstore, offs, offs2, offs3, offs4):
    idx = unstriped(offs)
    idx2 = unstriped(offs2)
    idx3 = unstriped(offs3)
    idx4 = unstriped(offs4)
    keysu = unpack_weight(keys_words, keys_scales, "e4m3")
    queryq = mxq(f64(query), 0, "e4m3")
    a = queryq.T @ keysu
    query2q = mxq(f64(query2), 0, "e4m3")
    pagesq = mxq(f64(pages), 0, "e4m3")
    h0 = query2q.T @ pagesq
    s = np.maximum(a[:, idx], h0[:, idx2]) - h0[:, idx3]
    w = sigmoid(s)
    wo1 = w * f64(os)
    wt1 = wo1.T
    vt1 = f64(vals)[:, idx].T
    vt1q = mxq(vt1, 0, "e4m3")
    wt1q = mxq(wt1, 0, "e4m3")
    wmq = mxq(f64(wm), 0, "e4m3")
    mstoreidx4q = mxq(f64(mstore)[:, idx4], 0, "e4m3")
    o = vt1q.T @ wt1q + wmq.T @ mstoreidx4q
    return o

@@ -1,0 +1,217 @@
+from contextlib import ExitStack
+
+import concourse.mybir as mybir
+from concourse.masks import make_identity
+
+D, T, I, Q, E, Z, M, C = 512, 2048, 512, 256, 512, 1024, 1024, 512
+FLOPS = 2 * (D * Q * T + D * Q * Z + I * E * Q + C * E * Q)
+
+F32 = mybir.dt.float32
+BF16 = mybir.dt.bfloat16
+I32 = mybir.dt.int32
+U32 = mybir.dt.uint32
+U16 = mybir.dt.uint16
+U8 = mybir.dt.uint8
+FP8X4 = mybir.dt.float8_e4m3fn_x4
+ALU = mybir.AluOpType
+ACT = mybir.ActivationFunctionType
+
+P = 128
+PACK = 4
+BANK = 512
+
+
+def tile_attend_largestof3_addedmemory_lean_kernel(
+    tc, query, query2, keys_words, keys_scales, pages, slot_factor, vals, wm, mstore,
+    offs, offs2, offs3, offs4, out,
+):
+    nc = tc.nc
+    with ExitStack() as ctx:
+        sb = ctx.enter_context(tc.tile_pool(name="sb", bufs=1))
+        acc_pool = ctx.enter_context(tc.psum_pool(name="acc", bufs=4))
+        turn_pool = ctx.enter_context(tc.psum_pool(name="turn", bufs=4))
+
+        def new(name, shape, dtype):
+            return sb.tile(shape, dtype, name=name, align_bytes=64)
+
+        def by_word(x):
+            return x.rearrange("(p t) n -> p t n", t=PACK)
+
+        q_raw = new("q_raw", [P, PACK, Q], F32)
+        q2_raw = new("q2_raw", [P, PACK, Q], F32)
+        key_codes = [new("key_codes%d" % h, [P, T // 2], U32) for h in range(2)]
+        key_scales = new("key_scales", [P, BANK], U8)
+        page_raw = [new("page_raw%d" % h, [P, PACK, BANK], F32) for h in range(2)]
+        mstore_raw = [new("mstore_raw%d" % t, [P, M], F32) for t in range(PACK)]
+        wm_raw = [new("wm_raw%d" % h, [P, PACK, E // 2], F32) for h in range(2)]
+        vals_raw = [new("vals_raw%d" % j, [P, T], F32) for j in range(E // P)]
+        factor = new("factor", [P, PACK], F32)
+        lst = new("lst", [P, I // 16], U16)
+        lst2 = new("lst2", [P, I // 16], U16)
+        lst3 = new("lst3", [P, I // 16], U16)
+        lst4 = new("lst4", [P, Q // 16], U16)
+        ident = new("ident", [P, P], F32)
+
+        key_words_hbm = keys_words[0].rearrange("p n t -> p (n t)").bitcast(I32)
+        key_scales_hbm = keys_scales[0].bitcast(I32)
+
+        nc.vector.memset(key_scales[:].bitcast(U32), 0)
+        nc.sync.dma_start(out=q_raw[:], in_=by_word(query))
+        for g in range(4):
+            nc.sync.dma_start(
+                out=key_scales[32 * g : 32 * g + 16, :].bitcast(I32),
+                in_=key_scales_hbm[4 * g : 4 * g + 4, :].rearrange("r (j c) -> j r c", j=4),
+            )
+        make_identity(nc, ident[:])
+
+        for h in range(2):
+            nc.sync.dma_start(out=key_codes[h][:].bitcast(I32), in_=key_words_hbm[:, h * T // 2 : (h + 1) * T // 2])
+        nc.sync.dma_start(out=q2_raw[:], in_=by_word(query2))
+        nc.sync.dma_start(out=page_raw[0][:], in_=by_word(pages)[:, :, 0:BANK])
+        nc.sync.dma_start(lst[:], offs)
+        nc.sync.dma_start(out=page_raw[1][:], in_=by_word(pages)[:, :, BANK:Z])
+        nc.sync.dma_start(lst4[:], offs4)
+        nc.sync.dma_start(out=mstore_raw[0][:], in_=by_word(mstore)[:, 0, :])
+        nc.sync.dma_start(lst2[:], offs2)
+        nc.sync.dma_start(out=mstore_raw[1][:], in_=by_word(mstore)[:, 1, :])
+        nc.sync.dma_start(lst3[:], offs3)
+        nc.sync.dma_start(out=mstore_raw[2][:], in_=by_word(mstore)[:, 2, :])
+        nc.sync.dma_start(out=factor[:], in_=slot_factor[0].rearrange("(p t) -> p t", t=PACK))
+        nc.sync.dma_start(out=mstore_raw[3][:], in_=by_word(mstore)[:, 3, :])
+        for j in range(E // P):
+            nc.sync.dma_start(out=vals_raw[j][:], in_=vals[j * P : (j + 1) * P, :])
+        for h in range(2):
+            nc.sync.dma_start(out=wm_raw[h][:], in_=by_word(wm)[:, :, h * E // 2 : (h + 1) * E // 2])
+
+        def weave_into(woven, raw, copy):
+            copy(
+                out=woven.rearrange("p (c i) t -> p c t i", i=4),
+                in_=raw.rearrange("p t (c i) -> p c t i", i=4),
+            )
+
+        def weave(name, raw, width, copy=nc.vector.tensor_copy):
+            woven = new(name + "_woven", [P, width, PACK], BF16)
+            weave_into(woven[:], raw, copy)
+            return woven
+
+        def mx_tiles(name, width):
+            return new(name + "_codes", [P, width], U32), new(name + "_scales", [P, width], U8)
+
+        def quantize(codes, scales, woven):
+            nc.vector.quantize_mx(out=codes.bitcast(FP8X4), scales=scales, in_=woven.rearrange("p n t -> p (n t)"))
+
+        def product(bank, lhs, lhs_scales, rhs, rhs_scales, start, stop):
+            nc.tensor.matmul_mx(
+                out=bank, lhsT=lhs.bitcast(FP8X4), lhsT_scale=lhs_scales,
+                rhs=rhs.bitcast(FP8X4), rhs_scale=rhs_scales, start=start, stop=stop,
+            )
+
+        rows = [slice(u * P, (u + 1) * P) for u in range(Q // P)]
+
+        q_codes, q_scales = mx_tiles("q", Q)
+        quantize(q_codes[:], q_scales[:], weave("q", q_raw[:], Q)[:])
+        a_sb = [new("a_sb%d" % u, [P, T], F32) for u in range(2)]
+        for u in range(2):
+            for j in range(T // BANK):
+                bank = acc_pool.tile([P, BANK], F32, name="acc")
+                h, c0 = divmod(j * BANK, T // 2)
+                product(bank[:], q_codes[:, rows[u]], q_scales[:, rows[u]],
+                        key_codes[h][:, c0 : c0 + BANK], key_scales[4 * j : P, :], True, True)
+                dst = a_sb[u][:, j * BANK : (j + 1) * BANK]
+                if u == 0 and j % 2 == 1:
+                    nc.vector.tensor_copy(out=dst, in_=bank[:])
+                else:
+                    nc.scalar.copy(out=dst, in_=bank[:])
+
+        q2_codes, q2_scales = mx_tiles("q2", Q)
+        quantize(q2_codes[:], q2_scales[:], weave("q2", q2_raw[:], Q)[:])
+
+        neg_a = [new("neg_a%d" % u, [P, I], F32) for u in range(2)]
+        nc.vector.tensor_scalar(neg_a[0][:], a_sb[0][:].indirect(lst[:]), -1.0, 0.0, ALU.mult, ALU.add)
+        nc.scalar.activation(neg_a[1][:], a_sb[1][:].indirect(lst[:]), ACT.Copy, scale=-1.0)
+
+        h_sb = [new("h_sb%d" % u, [P, Z], F32) for u in range(2)]
+        mem_picked = new("mem_picked", [P, PACK, Q], BF16)
+        for h in range(2):
+            page_codes, page_scales = mx_tiles("page%d" % h, BANK)
+            page_woven = new("page_woven%d" % h, [P, BANK, PACK], BF16)
+            cut = BANK - (0, 192)[h]
+            weave_into(page_woven[:, 0:cut, :], page_raw[h][:, :, 0:cut], nc.vector.tensor_copy)
+            if cut < BANK:
+                weave_into(page_woven[:, cut:BANK, :], page_raw[h][:, :, cut:BANK], nc.scalar.copy)
+            quantize(page_codes[:], page_scales[:], page_woven[:])
+            for u in range(2):
+                bank = acc_pool.tile([P, BANK], F32, name="acc")
+                product(bank[:], q2_codes[:, rows[u]], q2_scales[:, rows[u]], page_codes[:], page_scales[:], True, True)
+                dst = h_sb[u][:, h * BANK : (h + 1) * BANK]
+                if h == 1 and u == 1:
+                    nc.vector.tensor_copy(out=dst, in_=bank[:])
+                else:
+                    nc.scalar.copy(out=dst, in_=bank[:])
+
+        w_woven = new("w_woven", [P, Q, PACK], BF16)
+        w_codes, w_scales = mx_tiles("w", Q)
+        for u in range(2):
+            by2 = new("by2_%d" % u, [P, I], F32)
+            by3 = new("by3_%d" % u, [P, I], F32)
+            neg_max = new("neg_max%d" % u, [P, I], F32)
+            nc.scalar.activation(by3[:], h_sb[u][:].indirect(lst3[:]), ACT.Copy)
+            nc.vector.tensor_copy(by2[:], h_sb[u][:].indirect(lst2[:]))
+            nc.vector.scalar_tensor_tensor(neg_max[:], by2[:], -1.0, neg_a[u][:], ALU.mult, ALU.min)
+            bank = turn_pool.tile([P, PACK, P], F32, name="turn")
+            for n, term in enumerate((by3, neg_max)):
+                for t in range(PACK):
+                    nc.tensor.matmul(bank[:, t, :], lhsT=term[:, t : I : PACK], rhs=ident[:], is_transpose=True,
+                                     start=(n == 0 and t == 0), stop=(n == 1 and t == PACK - 1))
+            w_f32 = new("w_f32_%d" % u, [P, P, PACK], F32)
+            nc.scalar.activation(w_f32[:], bank[:].rearrange("p t q -> p q t"), ACT.Sigmoid, scale=-1.0)
+            nc.vector.tensor_tensor(w_woven[:, rows[u], :], w_f32[:],
+                                    factor[:].unsqueeze(1).to_broadcast([P, P, PACK]), ALU.mult)
+            quantize(w_codes[:, rows[u]], w_scales[:, rows[u]], w_woven[:, rows[u], :])
+
+        for t in range(PACK):
+            if t < 2:
+                nc.vector.tensor_copy(mem_picked[:, t, :], mstore_raw[t][:].indirect(lst4[:]))
+            else:
+                nc.scalar.activation(mem_picked[:, t, :], mstore_raw[t][:].indirect(lst4[:]), ACT.Copy)
+        mem_codes, mem_scales = mx_tiles("mem", Q)
+        quantize(mem_codes[:], mem_scales[:], weave("mem", mem_picked[:], Q)[:])
+
+        v_mx = []
+        out_bank = {}
+        for j in range(E // P):
+            picked = new("picked%d" % j, [P, I], BF16)
+            nc.scalar.activation(picked[:], vals_raw[j][:].indirect(lst[:]), ACT.Copy)
+            pairs = picked[:].bitcast(F32)
+            bank = turn_pool.tile([P, PACK, P], F32, name="turn")
+            for half in range(2):
+                nc.tensor.transpose(bank[:, half, :], pairs[:, half : I // 2 : 2], ident[:])
+            v_woven = new("v_woven%d" % j, [P, P, PACK], BF16)
+            copy = nc.scalar.copy if j == 3 else nc.vector.tensor_copy
+            copy(out=v_woven[:].bitcast(F32), in_=bank[:, 0:2, :].rearrange("p u e -> p e u"))
+            v_codes, v_scales = mx_tiles("v%d" % j, P)
+            quantize(v_codes[:], v_scales[:], v_woven[:])
+            v_mx.append((v_codes, v_scales))
+            if j >= 2:
+                out_bank[j] = acc_pool.tile([P, BANK], F32, name="acc")
+                product(out_bank[j][:, 0:Q], v_codes[:], v_scales[:], w_codes[:], w_scales[:], True, False)
+
+        feats = [slice(j * P, (j + 1) * P) for j in range(E // P)]
+        for j in range(E // P):
+            cols = slice((j % 2) * P, (j % 2 + 1) * P)
+            wm_woven = weave("wm%d" % j, wm_raw[j // 2][:, :, cols], P, nc.scalar.copy if j == 3 else nc.vector.tensor_copy)
+            wm_codes, wm_scales = mx_tiles("wm%d" % j, P)
+            quantize(wm_codes[:], wm_scales[:], wm_woven[:])
+            if j >= 2:
+                bank = out_bank[j]
+                product(bank[:, 0:Q], wm_codes[:], wm_scales[:], mem_codes[:], mem_scales[:], False, True)
+            else:
+                bank = acc_pool.tile([P, BANK], F32, name="acc")
+                product(bank[:, 0:Q], wm_codes[:], wm_scales[:], mem_codes[:], mem_scales[:], True, False)
+                product(bank[:, 0:Q], v_mx[j][0][:], v_mx[j][1][:], w_codes[:], w_scales[:], False, True)
+            result = new("result%d" % j, [P, Q], F32)
+            if j == 2:
+                nc.vector.tensor_copy(out=result[:], in_=bank[:, 0:Q])
+            else:
+                nc.scalar.copy(out=result[:], in_=bank[:, 0:Q])
+            nc.sync.dma_start(out=out[feats[j], :], in_=result[:])

@@ -56,6 +56,9 @@ def tile_attend_largestof3_addedmemory_lean_kernel(
         key_scales_hbm = keys_scales[0].bitcast(I32)
 
         nc.vector.memset(key_scales[:].bitcast(U32), 0)
+        warm = new("warm", [P, 2], F32)
+        nc.vector.memset(warm[:, 0:1], 0.0)
+        nc.scalar.activation(warm[:, 1:2], warm[:, 0:1], ACT.Sigmoid)
         nc.sync.dma_start(out=q_raw[:], in_=by_word(query))
         for g in range(4):
             nc.sync.dma_start(

@@ -67,22 +67,24 @@ def tile_attend_largestof3_addedmemory_lean_kernel(
             )
         make_identity(nc, ident[:])
 
-        for h in range(2):
+        def load_keys(h):
             nc.sync.dma_start(out=key_codes[h][:].bitcast(I32), in_=key_words_hbm[:, h * T // 2 : (h + 1) * T // 2])
+
+        load_keys(0)
         nc.sync.dma_start(out=q2_raw[:], in_=by_word(query2))
-        nc.sync.dma_start(out=page_raw[0][:], in_=by_word(pages)[:, :, 0:BANK])
+        load_keys(1)
         nc.sync.dma_start(lst[:], offs)
+        nc.sync.dma_start(out=page_raw[0][:], in_=by_word(pages)[:, :, 0:BANK])
         nc.sync.dma_start(out=page_raw[1][:], in_=by_word(pages)[:, :, BANK:Z])
         nc.sync.dma_start(lst4[:], offs4)
-        nc.sync.dma_start(out=mstore_raw[0][:], in_=by_word(mstore)[:, 0, :])
-        nc.sync.dma_start(lst2[:], offs2)
-        nc.sync.dma_start(out=mstore_raw[1][:], in_=by_word(mstore)[:, 1, :])
-        nc.sync.dma_start(lst3[:], offs3)
-        nc.sync.dma_start(out=mstore_raw[2][:], in_=by_word(mstore)[:, 2, :])
-        nc.sync.dma_start(out=factor[:], in_=slot_factor[0].rearrange("(p t) -> p t", t=PACK))
-        nc.sync.dma_start(out=mstore_raw[3][:], in_=by_word(mstore)[:, 3, :])
-        for j in range(E // P):
+        for j in range(PACK):
+            nc.sync.dma_start(out=mstore_raw[j][:], in_=by_word(mstore)[:, j, :])
+            if j == 0:
+                nc.sync.dma_start(lst3[:], offs3)
+                nc.sync.dma_start(lst2[:], offs2)
             nc.sync.dma_start(out=vals_raw[j][:], in_=vals[j * P : (j + 1) * P, :])
+            if j == 0:
+                nc.sync.dma_start(out=factor[:], in_=slot_factor[0].rearrange("(p t) -> p t", t=PACK))
         for h in range(2):
             nc.sync.dma_start(out=wm_raw[h][:], in_=by_word(wm)[:, :, h * E // 2 : (h + 1) * E // 2])
 
@@ -130,15 +132,15 @@ def tile_attend_largestof3_addedmemory_lean_kernel(
         quantize(q2_codes[:], q2_scales[:], weave("q2", q2_raw[:], Q)[:])
 
         neg_a = [new("neg_a%d" % u, [P, I], F32) for u in range(2)]
-        nc.vector.tensor_scalar(neg_a[0][:], a_sb[0][:].indirect(lst[:]), -1.0, 0.0, ALU.mult, ALU.add)
-        nc.scalar.activation(neg_a[1][:], a_sb[1][:].indirect(lst[:]), ACT.Copy, scale=-1.0)
+        for u in range(2):
+            nc.scalar.activation(neg_a[u][:], a_sb[u][:].indirect(lst[:]), ACT.Copy, scale=-1.0)
 
         h_sb = [new("h_sb%d" % u, [P, Z], F32) for u in range(2)]
         mem_picked = new("mem_picked", [P, PACK, Q], BF16)
         for h in range(2):
             page_codes, page_scales = mx_tiles("page%d" % h, BANK)
             page_woven = new("page_woven%d" % h, [P, BANK, PACK], BF16)
-            cut = BANK - (0, 192)[h]
+            cut = BANK - (0, 0)[h]
             weave_into(page_woven[:, 0:cut, :], page_raw[h][:, :, 0:cut], nc.vector.tensor_copy)
             if cut < BANK:
                 weave_into(page_woven[:, cut:BANK, :], page_raw[h][:, :, cut:BANK], nc.scalar.copy)
@@ -147,7 +149,7 @@ def tile_attend_largestof3_addedmemory_lean_kernel(
                 bank = acc_pool.tile([P, BANK], F32, name="acc")
                 product(bank[:], q2_codes[:, rows[u]], q2_scales[:, rows[u]], page_codes[:], page_scales[:], True, True)
                 dst = h_sb[u][:, h * BANK : (h + 1) * BANK]
-                if h == 1 and u == 1:
+                if h == 1:
                     nc.vector.tensor_copy(out=dst, in_=bank[:])
                 else:
                     nc.scalar.copy(out=dst, in_=bank[:])
@@ -157,15 +159,20 @@ def tile_attend_largestof3_addedmemory_lean_kernel(
         for u in range(2):
             by2 = new("by2_%d" % u, [P, I], F32)
             by3 = new("by3_%d" % u, [P, I], F32)
-            neg_max = new("neg_max%d" % u, [P, I], F32)
+            neg_max = new("neg_max%d" % u, [P, PACK, P], F32)
             nc.scalar.activation(by3[:], h_sb[u][:].indirect(lst3[:]), ACT.Copy)
             nc.vector.tensor_copy(by2[:], h_sb[u][:].indirect(lst2[:]))
-            nc.vector.scalar_tensor_tensor(neg_max[:], by2[:], -1.0, neg_a[u][:], ALU.mult, ALU.min)
+            nc.vector.scalar_tensor_tensor(
+                neg_max[:].rearrange("q t s -> q s t"), by2[:].rearrange("q (s t) -> q s t", t=PACK), -1.0,
+                neg_a[u][:].rearrange("q (s t) -> q s t", t=PACK), ALU.mult, ALU.min,
+            )
             bank = turn_pool.tile([P, PACK, P], F32, name="turn")
-            for n, term in enumerate((by3, neg_max)):
-                for t in range(PACK):
-                    nc.tensor.matmul(bank[:, t, :], lhsT=term[:, t : I : PACK], rhs=ident[:], is_transpose=True,
-                                     start=(n == 0 and t == 0), stop=(n == 1 and t == PACK - 1))
+            for t in range(PACK):
+                nc.tensor.matmul(bank[:, t, :], lhsT=by3[:, t : I : PACK], rhs=ident[:], is_transpose=True,
+                                 start=(t == 0), stop=False)
+            for t in range(PACK):
+                nc.tensor.matmul(bank[:, t, :], lhsT=neg_max[:, t, :], rhs=ident[:], is_transpose=True,
+                                 start=False, stop=(t == PACK - 1))
             w_f32 = new("w_f32_%d" % u, [P, P, PACK], F32)
             nc.scalar.activation(w_f32[:], bank[:].rearrange("p t q -> p q t"), ACT.Sigmoid, scale=-1.0)
             nc.vector.tensor_tensor(w_woven[:, rows[u], :], w_f32[:],
@@ -173,7 +180,7 @@ def tile_attend_largestof3_addedmemory_lean_kernel(
             quantize(w_codes[:, rows[u]], w_scales[:, rows[u]], w_woven[:, rows[u], :])
 
         for t in range(PACK):
-            if t < 2:
+            if t < 3:
                 nc.vector.tensor_copy(mem_picked[:, t, :], mstore_raw[t][:].indirect(lst4[:]))
             else:
                 nc.scalar.activation(mem_picked[:, t, :], mstore_raw[t][:].indirect(lst4[:]), ACT.Copy)
@@ -190,7 +197,7 @@ def tile_attend_largestof3_addedmemory_lean_kernel(
             for half in range(2):
                 nc.tensor.transpose(bank[:, half, :], pairs[:, half : I // 2 : 2], ident[:])
             v_woven = new("v_woven%d" % j, [P, P, PACK], BF16)
-            copy = nc.scalar.copy if j == 3 else nc.vector.tensor_copy
+            copy = nc.vector.tensor_copy
             copy(out=v_woven[:].bitcast(F32), in_=bank[:, 0:2, :].rearrange("p u e -> p e u"))
             v_codes, v_scales = mx_tiles("v%d" % j, P)
             quantize(v_codes[:], v_scales[:], v_woven[:])
@@ -202,7 +209,7 @@ def tile_attend_largestof3_addedmemory_lean_kernel(
         feats = [slice(j * P, (j + 1) * P) for j in range(E // P)]
         for j in range(E // P):
             cols = slice((j % 2) * P, (j % 2 + 1) * P)
-            wm_woven = weave("wm%d" % j, wm_raw[j // 2][:, :, cols], P, nc.scalar.copy if j == 3 else nc.vector.tensor_copy)
+            wm_woven = weave("wm%d" % j, wm_raw[j // 2][:, :, cols], P, nc.scalar.copy if j < 3 else nc.vector.tensor_copy)
             wm_codes, wm_scales = mx_tiles("wm%d" % j, P)
             quantize(wm_codes[:], wm_scales[:], wm_woven[:])
             if j >= 2:
@@ -213,7 +220,7 @@ def tile_attend_largestof3_addedmemory_lean_kernel(
                 product(bank[:, 0:Q], wm_codes[:], wm_scales[:], mem_codes[:], mem_scales[:], True, False)
                 product(bank[:, 0:Q], v_mx[j][0][:], v_mx[j][1][:], w_codes[:], w_scales[:], False, True)
             result = new("result%d" % j, [P, Q], F32)
-            if j == 2:
+            if j == 3:
                 nc.vector.tensor_copy(out=result[:], in_=bank[:, 0:Q])
             else:
                 nc.scalar.copy(out=result[:], in_=bank[:, 0:Q])

from contextlib import ExitStack

import concourse.mybir as mybir
from concourse.masks import make_identity

D, T, I, Q, E, Z, M, C = 512, 2048, 512, 256, 512, 1024, 1024, 512
FLOPS = 2 * (D * Q * T + D * Q * Z + I * E * Q + C * E * Q)

F32 = mybir.dt.float32
BF16 = mybir.dt.bfloat16
I32 = mybir.dt.int32
U32 = mybir.dt.uint32
U16 = mybir.dt.uint16
U8 = mybir.dt.uint8
FP8X4 = mybir.dt.float8_e4m3fn_x4
ALU = mybir.AluOpType
ACT = mybir.ActivationFunctionType

P = 128
PACK = 4
BANK = 512


def tile_attend_largestof3_addedmemory_lean_kernel(
    tc, query, query2, keys_words, keys_scales, pages, slot_factor, vals, wm, mstore,
    offs, offs2, offs3, offs4, out,
):
    nc = tc.nc
    with ExitStack() as ctx:
        sb = ctx.enter_context(tc.tile_pool(name="sb", bufs=1))
        acc_pool = ctx.enter_context(tc.psum_pool(name="acc", bufs=4))
        turn_pool = ctx.enter_context(tc.psum_pool(name="turn", bufs=4))

        def new(name, shape, dtype):
            return sb.tile(shape, dtype, name=name, align_bytes=64)

        def by_word(x):
            return x.rearrange("(p t) n -> p t n", t=PACK)

        q_raw = new("q_raw", [P, PACK, Q], F32)
        q2_raw = new("q2_raw", [P, PACK, Q], F32)
        key_codes = [new("key_codes%d" % h, [P, T // 2], U32) for h in range(2)]
        key_scales = new("key_scales", [P, BANK], U8)
        page_raw = [new("page_raw%d" % h, [P, PACK, BANK], F32) for h in range(2)]
        mstore_raw = [new("mstore_raw%d" % t, [P, M], F32) for t in range(PACK)]
        wm_raw = [new("wm_raw%d" % h, [P, PACK, E // 2], F32) for h in range(2)]
        vals_raw = [new("vals_raw%d" % j, [P, T], F32) for j in range(E // P)]
        factor = new("factor", [P, PACK], F32)
        lst = new("lst", [P, I // 16], U16)
        lst2 = new("lst2", [P, I // 16], U16)
        lst3 = new("lst3", [P, I // 16], U16)
        lst4 = new("lst4", [P, Q // 16], U16)
        ident = new("ident", [P, P], F32)

        key_words_hbm = keys_words[0].rearrange("p n t -> p (n t)").bitcast(I32)
        key_scales_hbm = keys_scales[0].bitcast(I32)

        nc.vector.memset(key_scales[:].bitcast(U32), 0)
        warm = new("warm", [P, 2], F32)
        nc.vector.memset(warm[:, 0:1], 0.0)
        nc.scalar.activation(warm[:, 1:2], warm[:, 0:1], ACT.Sigmoid)
        nc.sync.dma_start(out=q_raw[:], in_=by_word(query))
        for g in range(4):
            nc.sync.dma_start(
                out=key_scales[32 * g : 32 * g + 16, :].bitcast(I32),
                in_=key_scales_hbm[4 * g : 4 * g + 4, :].rearrange("r (j c) -> j r c", j=4),
            )
        make_identity(nc, ident[:])

        def load_keys(h):
            nc.sync.dma_start(out=key_codes[h][:].bitcast(I32), in_=key_words_hbm[:, h * T // 2 : (h + 1) * T // 2])

        load_keys(0)
        nc.sync.dma_start(out=q2_raw[:], in_=by_word(query2))
        load_keys(1)
        nc.sync.dma_start(lst[:], offs)
        nc.sync.dma_start(out=page_raw[0][:], in_=by_word(pages)[:, :, 0:BANK])
        nc.sync.dma_start(out=page_raw[1][:], in_=by_word(pages)[:, :, BANK:Z])
        nc.sync.dma_start(lst4[:], offs4)
        for j in range(PACK):
            nc.sync.dma_start(out=mstore_raw[j][:], in_=by_word(mstore)[:, j, :])
            if j == 0:
                nc.sync.dma_start(lst3[:], offs3)
                nc.sync.dma_start(lst2[:], offs2)
            nc.sync.dma_start(out=vals_raw[j][:], in_=vals[j * P : (j + 1) * P, :])
            if j == 0:
                nc.sync.dma_start(out=factor[:], in_=slot_factor[0].rearrange("(p t) -> p t", t=PACK))
        for h in range(2):
            nc.sync.dma_start(out=wm_raw[h][:], in_=by_word(wm)[:, :, h * E // 2 : (h + 1) * E // 2])

        def weave_into(woven, raw, copy):
            copy(
                out=woven.rearrange("p (c i) t -> p c t i", i=4),
                in_=raw.rearrange("p t (c i) -> p c t i", i=4),
            )

        def weave(name, raw, width, copy=nc.vector.tensor_copy):
            woven = new(name + "_woven", [P, width, PACK], BF16)
            weave_into(woven[:], raw, copy)
            return woven

        def mx_tiles(name, width):
            return new(name + "_codes", [P, width], U32), new(name + "_scales", [P, width], U8)

        def quantize(codes, scales, woven):
            nc.vector.quantize_mx(out=codes.bitcast(FP8X4), scales=scales, in_=woven.rearrange("p n t -> p (n t)"))

        def product(bank, lhs, lhs_scales, rhs, rhs_scales, start, stop):
            nc.tensor.matmul_mx(
                out=bank, lhsT=lhs.bitcast(FP8X4), lhsT_scale=lhs_scales,
                rhs=rhs.bitcast(FP8X4), rhs_scale=rhs_scales, start=start, stop=stop,
            )

        rows = [slice(u * P, (u + 1) * P) for u in range(Q // P)]

        q_codes, q_scales = mx_tiles("q", Q)
        quantize(q_codes[:], q_scales[:], weave("q", q_raw[:], Q)[:])
        a_sb = [new("a_sb%d" % u, [P, T], F32) for u in range(2)]
        for u in range(2):
            for j in range(T // BANK):
                bank = acc_pool.tile([P, BANK], F32, name="acc")
                h, c0 = divmod(j * BANK, T // 2)
                product(bank[:], q_codes[:, rows[u]], q_scales[:, rows[u]],
                        key_codes[h][:, c0 : c0 + BANK], key_scales[4 * j : P, :], True, True)
                dst = a_sb[u][:, j * BANK : (j + 1) * BANK]
                if u == 0 and j % 2 == 1:
                    nc.vector.tensor_copy(out=dst, in_=bank[:])
                else:
                    nc.scalar.copy(out=dst, in_=bank[:])

        q2_codes, q2_scales = mx_tiles("q2", Q)
        quantize(q2_codes[:], q2_scales[:], weave("q2", q2_raw[:], Q)[:])

        neg_a = [new("neg_a%d" % u, [P, I], F32) for u in range(2)]
        for u in range(2):
            nc.scalar.activation(neg_a[u][:], a_sb[u][:].indirect(lst[:]), ACT.Copy, scale=-1.0)

        h_sb = [new("h_sb%d" % u, [P, Z], F32) for u in range(2)]
        mem_picked = new("mem_picked", [P, PACK, Q], BF16)
        for h in range(2):
            page_codes, page_scales = mx_tiles("page%d" % h, BANK)
            page_woven = new("page_woven%d" % h, [P, BANK, PACK], BF16)
            cut = BANK - (0, 0)[h]
            weave_into(page_woven[:, 0:cut, :], page_raw[h][:, :, 0:cut], nc.vector.tensor_copy)
            if cut < BANK:
                weave_into(page_woven[:, cut:BANK, :], page_raw[h][:, :, cut:BANK], nc.scalar.copy)
            quantize(page_codes[:], page_scales[:], page_woven[:])
            for u in range(2):
                bank = acc_pool.tile([P, BANK], F32, name="acc")
                product(bank[:], q2_codes[:, rows[u]], q2_scales[:, rows[u]], page_codes[:], page_scales[:], True, True)
                dst = h_sb[u][:, h * BANK : (h + 1) * BANK]
                if h == 1:
                    nc.vector.tensor_copy(out=dst, in_=bank[:])
                else:
                    nc.scalar.copy(out=dst, in_=bank[:])

        w_woven = new("w_woven", [P, Q, PACK], BF16)
        w_codes, w_scales = mx_tiles("w", Q)
        for u in range(2):
            by2 = new("by2_%d" % u, [P, I], F32)
            by3 = new("by3_%d" % u, [P, I], F32)
            neg_max = new("neg_max%d" % u, [P, PACK, P], F32)
            nc.scalar.activation(by3[:], h_sb[u][:].indirect(lst3[:]), ACT.Copy)
            nc.vector.tensor_copy(by2[:], h_sb[u][:].indirect(lst2[:]))
            nc.vector.scalar_tensor_tensor(
                neg_max[:].rearrange("q t s -> q s t"), by2[:].rearrange("q (s t) -> q s t", t=PACK), -1.0,
                neg_a[u][:].rearrange("q (s t) -> q s t", t=PACK), ALU.mult, ALU.min,
            )
            bank = turn_pool.tile([P, PACK, P], F32, name="turn")
            for t in range(PACK):
                nc.tensor.matmul(bank[:, t, :], lhsT=by3[:, t : I : PACK], rhs=ident[:], is_transpose=True,
                                 start=(t == 0), stop=False)
            for t in range(PACK):
                nc.tensor.matmul(bank[:, t, :], lhsT=neg_max[:, t, :], rhs=ident[:], is_transpose=True,
                                 start=False, stop=(t == PACK - 1))
            w_f32 = new("w_f32_%d" % u, [P, P, PACK], F32)
            nc.scalar.activation(w_f32[:], bank[:].rearrange("p t q -> p q t"), ACT.Sigmoid, scale=-1.0)
            nc.vector.tensor_tensor(w_woven[:, rows[u], :], w_f32[:],
                                    factor[:].unsqueeze(1).to_broadcast([P, P, PACK]), ALU.mult)
            quantize(w_codes[:, rows[u]], w_scales[:, rows[u]], w_woven[:, rows[u], :])

        for t in range(PACK):
            if t < 3:
                nc.vector.tensor_copy(mem_picked[:, t, :], mstore_raw[t][:].indirect(lst4[:]))
            else:
                nc.scalar.activation(mem_picked[:, t, :], mstore_raw[t][:].indirect(lst4[:]), ACT.Copy)
        mem_codes, mem_scales = mx_tiles("mem", Q)
        quantize(mem_codes[:], mem_scales[:], weave("mem", mem_picked[:], Q)[:])

        v_mx = []
        out_bank = {}
        for j in range(E // P):
            picked = new("picked%d" % j, [P, I], BF16)
            nc.scalar.activation(picked[:], vals_raw[j][:].indirect(lst[:]), ACT.Copy)
            pairs = picked[:].bitcast(F32)
            bank = turn_pool.tile([P, PACK, P], F32, name="turn")
            for half in range(2):
                nc.tensor.transpose(bank[:, half, :], pairs[:, half : I // 2 : 2], ident[:])
            v_woven = new("v_woven%d" % j, [P, P, PACK], BF16)
            copy = nc.vector.tensor_copy
            copy(out=v_woven[:].bitcast(F32), in_=bank[:, 0:2, :].rearrange("p u e -> p e u"))
            v_codes, v_scales = mx_tiles("v%d" % j, P)
            quantize(v_codes[:], v_scales[:], v_woven[:])
            v_mx.append((v_codes, v_scales))
            if j >= 2:
                out_bank[j] = acc_pool.tile([P, BANK], F32, name="acc")
                product(out_bank[j][:, 0:Q], v_codes[:], v_scales[:], w_codes[:], w_scales[:], True, False)

        feats = [slice(j * P, (j + 1) * P) for j in range(E // P)]
        for j in range(E // P):
            cols = slice((j % 2) * P, (j % 2 + 1) * P)
            wm_woven = weave("wm%d" % j, wm_raw[j // 2][:, :, cols], P, nc.scalar.copy if j < 3 else nc.vector.tensor_copy)
            wm_codes, wm_scales = mx_tiles("wm%d" % j, P)
            quantize(wm_codes[:], wm_scales[:], wm_woven[:])
            if j >= 2:
                bank = out_bank[j]
                product(bank[:, 0:Q], wm_codes[:], wm_scales[:], mem_codes[:], mem_scales[:], False, True)
            else:
                bank = acc_pool.tile([P, BANK], F32, name="acc")
                product(bank[:, 0:Q], wm_codes[:], wm_scales[:], mem_codes[:], mem_scales[:], True, False)
                product(bank[:, 0:Q], v_mx[j][0][:], v_mx[j][1][:], w_codes[:], w_scales[:], False, True)
            result = new("result%d" % j, [P, Q], F32)
            if j == 3:
                nc.vector.tensor_copy(out=result[:], in_=bank[:, 0:Q])
            else:
                nc.scalar.copy(out=result[:], in_=bank[:, 0:Q])
            nc.sync.dma_start(out=out[feats[j], :], in_=result[:])
